import numpy as np, ml_dtypes
CORES = [10,34,74,98]
N = 4
import mx_ref
NC, G = 128, 2
C = np.float32(0.047)
BF = ml_dtypes.bfloat16
def cut(t, i, w=512):
    return t[:, w * i:w * i + w]
def tile(rs):
    return np.stack(rs, axis=2).reshape(128, -1).astype(BF)
def layer(w, X):
    out = []
    for i in range(G):
        for t in range(len(X)):
            p = mx_ref.matmul(mx_ref.quantize(cut(w, len(X) * i + t)), X[t])
            z = p if t == 0 else z + p
        out.append(z)
    return out
def act(Z):
    return [np.maximum(s * z, 0) * C for z in Z for s in (1, -1)]
def setup_inputs(rng):
    def f(*shape):
        return mx_ref.flush((rng.standard_normal(shape, dtype=np.float32) * np.exp2(rng.integers(-2, 3, shape[:-1] + (1,)))).astype(BF))
    return {"x": f(N, 128, 4 * NC), "w1": f(N, 128, G * 512), "w2": f(N, 128, 512)}
def setup_inputs_blocks(rng):
    d = setup_inputs(rng)
    for k in ("x", "w1", "w2"): d[k] = mx_ref.spread(d[k], rng, 2)
    return d
def setup_inputs_wide(rng):
    d = setup_inputs(rng)
    for k in ("x", "w1", "w2"): d[k] = mx_ref.flush((d[k].astype(np.float32) * np.exp2(rng.integers(-6, 7, (N, 1, 1))).astype(np.float32)).astype(BF))
    return d
def reference(x, w1, w2):
    X = [mx_ref.quantize(x[j]) for j in range(N)]
    y = np.zeros((N, 128, NC), np.float32)
    for c in range(N):
        for r in range(N):
            p = mx_ref.matmul(mx_ref.quantize(w2[r]), mx_ref.quantize(tile(act(layer(w1[r], [X[c]])))))
            y[c] = p if r == 0 else y[c] + p
    return {"y": y}

@@ -1,0 +1,208 @@
+from concourse.bass import DstId, RemoteDMATransfer
+from concourse.mybir import dt, AluOpType, ActivationFunctionType
+
+N = 4
+NSIM = 112
+NC = 128
+SLOT = 3 * NC
+C = 0.047
+
+PIECES = {
+    "w1a": ("c", 0, NC, "A"),
+    "w1b": ("c", NC, 2 * NC, "A"),
+    "w2": ("c", 2 * NC, 3 * NC, "B"),
+    "sc": ("s", 0, 3 * NC, "A"),
+}
+STEPS = [
+    (1, [("w1a", ("far", 0), "hiL"), ("w1b", ("far", 1), "hiH")]),
+    (2, [("w2", ("near", 0), "lo")]),
+    (2, [("sc", "all", "lo")]),
+]
+ZSET = [0, 1, 2, 0]
+
+SCRATCH = {
+    "wb": ("sbuf", [128, 4 * SLOT], "bfloat16"),
+    "xb": ("sbuf", [128, 4 * NC], "bfloat16"),
+    "wq": ("sbuf", [128, N * SLOT], "float8_e4m3fn_x4"),
+    "ws": ("sbuf", [128, N * SLOT], "uint8"),
+    "xq": ("sbuf", [128, NC], "float8_e4m3fn_x4"),
+    "xs": ("sbuf", [128, NC], "uint8"),
+    "hb": ("sbuf", [128, N * 4 * NC], "bfloat16"),
+    "hq": ("sbuf", [128, N * NC], "float8_e4m3fn_x4"),
+    "hs": ("sbuf", [128, N * NC], "uint8"),
+    "yb": ("sbuf", [128, NC], "float32"),
+    "pz": ("psum", [128, 512 * 6], "float32"),
+    "py": ("psum", [128, 512], "float32"),
+}
+SEMAPHORES = (["ldw1", "ldw2", "ldx", "qw1", "qw2", "qx", "yd", "yc", "st", "sent"]
+              + ["in_" + p for p in PIECES]
+              + ["arr%s%d" % (c, s) for c in "AB" for s in range(N)]
+              + ["%s%d" % (n, k) for n in ("za", "zb", "hr", "hd") for k in range(N)])
+
+
+def _engines(mask):
+    return [e for e in range(mask.bit_length()) if (mask >> e) & 1]
+
+
+def _mask(es):
+    m = 0
+    for e in es:
+        m |= 1 << e
+    return m
+
+
+def _carriers(rc, group, topo):
+    others = [d for d in group if d != rc]
+    cs = [c for c in range(NSIM) if topo.chip(c) == topo.chip(rc) and c not in group
+          and all(topo.may_write(c, d) for d in others)]
+    return {"far": [c for c in cs if topo.die(c) != topo.die(rc)],
+            "near": [c for c in cs if topo.die(c) == topo.die(rc)]}
+
+
+def _parts(src, on_chip, off_chip, topo):
+    lo = _engines(topo.mask(src, off_chip))
+    hi = [e for e in _engines(topo.mask(src, on_chip)) if e not in lo]
+    return {"lo": lo, "hi": hi, "all": lo + hi,
+            "loL": lo[:len(lo) // 2], "loH": lo[len(lo) // 2:], "hiL": hi[:len(hi) // 2], "hiH": hi[len(hi) // 2:]}
+
+
+def _view(T, piece, s):
+    kind, a, b, _ = PIECES[piece]
+    if kind == "c":
+        return T.wq[:, s * SLOT + a:s * SLOT + b].bitcast(dt.uint8)
+    return T.ws[:, s * SLOT + a:s * SLOT + b]
+
+
+def _transfer(T, topo, piece, s, dsts, es, sem):
+    return RemoteDMATransfer(dst_ids=[DstId(rid=topo.addr(d)[0], pnc=topo.addr(d)[1]) for d in dsts],
+                             dma_engine_mask=_mask(es), remote_sem=sem,
+                             srcs=[_view(T, piece, s)], dsts=[_view(T, piece, s) for d in dsts])
+
+
+def _arr(T, piece, s):
+    return T.sem["arr%s%d" % (PIECES[piece][3], s)]
+
+
+def _after(group, s):
+    return [group[(s + k) % N] for k in range(1, N)]
+
+
+def carrier_program(g, core, T, topo, group, s):
+    rc = group[s]
+    cs = _carriers(rc, group, topo)
+    dsts = _after(group, s)
+    give = _parts(rc, core, dsts[0], topo)
+    lo = _parts(core, rc, dsts[0], topo)["lo"]
+    sent = 0
+    for _, trs in STEPS:
+        for piece, to, part in trs:
+            if to != "all" and cs[to[0]][to[1]] == core:
+                g.wait_ge(T.sem["in_" + piece], len(give[part]))
+                g.remote_dma_fused([_transfer(T, topo, piece, s, dsts, lo, _arr(T, piece, s))], local_sem=T.sem.sent)
+                sent += len(lo)
+    if sent:
+        g.wait_ge(T.sem.sent, sent)
+
+
+def rank_program(g, core, T, topo):
+    group = [int(c) for c in T.cores]
+    me = T.rank_of(core)
+    if me is None:
+        for s in range(N):
+            if topo.chip(group[s]) == topo.chip(core):
+                carrier_program(g, core, T, topo, group, s)
+        return
+    S = T.sem
+    own = me * SLOT
+
+    g.sync.dma_start(T.wb[:, 0:8 * NC], T.w1[:]).then_inc(S.ldw1, 16)
+    g.scalar.dma_start(T.wb[:, 8 * NC:12 * NC], T.w2[:]).then_inc(S.ldw2, 16)
+    g.sync.dma_start(T.xb[:], T.x[:]).then_inc(S.ldx, 16)
+
+    g.vector.wait_ge(S.ldw1, 16)
+    g.vector.quantize_mx(T.wq[:, own:own + 2 * NC], T.ws[:, own:own + 2 * NC], T.wb[:, 0:8 * NC]).then_inc(S.qw1, 1)
+    g.vector.wait_ge(S.ldw2, 16)
+    g.vector.quantize_mx(T.wq[:, own + 2 * NC:own + SLOT], T.ws[:, own + 2 * NC:own + SLOT],
+                         T.wb[:, 8 * NC:12 * NC]).then_inc(S.qw2, 1)
+    g.vector.wait_ge(S.ldx, 16)
+    g.vector.quantize_mx(T.xq[:], T.xs[:], T.xb[:]).then_inc(S.qx, 1)
+
+    cs = _carriers(core, group, topo)
+    dsts = _after(group, me)
+    parts = _parts(core, (cs["far"] + cs["near"])[0], dsts[0], topo)
+    stage, sent = 0, 0
+    for st, trs in STEPS:
+        while stage < st:
+            stage += 1
+            g.wait_ge(S["qw%d" % stage], 1)
+        call = []
+        for piece, to, part in trs:
+            if to == "all":
+                call.append(_transfer(T, topo, piece, me, dsts, parts[part], _arr(T, piece, me)))
+            else:
+                call.append(_transfer(T, topo, piece, me, [cs[to[0]][to[1]]], parts[part], S["in_" + piece]))
+            sent += len(parts[part])
+        g.remote_dma_fused(call, local_sem=S.sent)
+    g.wait_ge(S.sent, sent)
+
+    need = {"A": 0, "B": 0}
+    for _, trs in STEPS:
+        for piece, to, part in trs:
+            need[PIECES[piece][3]] += len(parts[part] if to == "all" else parts["lo"])
+
+    order = [(me - k) % N for k in range(N)]
+
+    def bank(k, i):
+        b = 512 * (2 * ZSET[k] + i)
+        return T.pz[:, b:b + NC]
+
+    def z(k):
+        a = order[k] * SLOT
+        if k == 0:
+            g.tensor.wait_ge(S.qw1, 1)
+            g.tensor.wait_ge(S.qx, 1)
+        else:
+            g.tensor.wait_ge(S["arrA%d" % order[k]], need["A"])
+        for i, n in enumerate(("za", "zb")):
+            g.tensor.matmul_mx(bank(k, i), T.wq[:, a + i * NC:a + (i + 1) * NC], T.ws[:, a + i * NC:a + (i + 1) * NC],
+                               T.xq[:], T.xs[:], True, True).then_inc(S["%s%d" % (n, k)], 1)
+
+    def y(k, first, last):
+        a = order[k] * SLOT + 2 * NC
+        if k == 0:
+            g.tensor.wait_ge(S.qw2, 1)
+        elif need["B"]:
+            g.tensor.wait_ge(S["arrB%d" % order[k]], need["B"])
+        g.tensor.wait_ge(S["hd%d" % k], 1)
+        mm = g.tensor.matmul_mx(T.py[:, 0:NC], T.wq[:, a:a + NC], T.ws[:, a:a + NC],
+                                T.hq[:, k * NC:(k + 1) * NC], T.hs[:, k * NC:(k + 1) * NC], first, last)
+        if last:
+            mm.then_inc(S.yd, 1)
+
+    z(0)
+    y(0, True, False)
+    z(1)
+    z(2)
+    y(1, False, False)
+    z(3)
+    y(2, False, False)
+    y(3, False, True)
+
+    for k in range(N):
+        h = k * 4 * NC
+        hr = S["hr%d" % k]
+        g.vector.wait_ge(S["za%d" % k], 1)
+        g.vector.tensor_scalar(T.hb[:, h + 0:h + 4 * NC:4], bank(k, 0), C, 0.0, AluOpType.mult, AluOpType.max).then_inc(hr, 1)
+        g.vector.tensor_scalar(T.hb[:, h + 1:h + 4 * NC:4], bank(k, 0), -C, 0.0, AluOpType.mult, AluOpType.max).then_inc(hr, 1)
+        g.scalar.wait_ge(S["zb%d" % k], 1)
+        g.scalar.activation(T.hb[:, h + 2:h + 4 * NC:4], bank(k, 1), ActivationFunctionType.Relu, scale=C).then_inc(hr, 1)
+        g.scalar.activation(T.hb[:, h + 3:h + 4 * NC:4], bank(k, 1), ActivationFunctionType.Relu, scale=-C).then_inc(hr, 1)
+        g.vector.wait_ge(hr, 4)
+        g.vector.quantize_mx(T.hq[:, k * NC:(k + 1) * NC], T.hs[:, k * NC:(k + 1) * NC],
+                             T.hb[:, h:h + 4 * NC]).then_inc(S["hd%d" % k], 1)
+
+    g.vector.wait_ge(S.yd, 1)
+    g.vector.tensor_copy(T.yb[:], T.py[:, 0:NC]).then_inc(S.yc, 1)
+    g.sync.wait_ge(S.yc, 1)
+    g.sync.dma_start(T.y[:], T.yb[:]).then_inc(S.st, 16)
+    g.sync.wait_ge(S.st, 16)

@@ -14,9 +14,11 @@ PIECES = {
     "sc": ("s", 0, 3 * NC, "A"),
 }
 STEPS = [
-    (1, [("w1a", ("far", 0), "hiL"), ("w1b", ("far", 1), "hiH")]),
-    (2, [("w2", ("near", 0), "lo")]),
-    (2, [("sc", "all", "lo")]),
+    (1, [("w1a", ("far", 0), "hi"), ("w1a", "plane", "lo")]),
+    (2, [("w1b", ("far", 1), "hi"), ("w1b", "plane", "lo")]),
+    (3, [("w2", ("near", 0), "hi")]),
+    (3, [("sc", "ranks", "lo")]),
+    (3, [("w2", "plane", "lo")]),
 ]
 ZSET = [0, 1, 2, 0]
 
@@ -34,7 +36,7 @@ SCRATCH = {
     "pz": ("psum", [128, 512 * 6], "float32"),
     "py": ("psum", [128, 512], "float32"),
 }
-SEMAPHORES = (["ldw1", "ldw2", "ldx", "qw1", "qw2", "qx", "yd", "yc", "st", "sent"]
+SEMAPHORES = (["ld1", "ld2", "ld3", "ldx", "qw1", "qw2", "qw3", "qx", "yd", "yc", "st", "sent"]
               + ["in_" + p for p in PIECES]
               + ["arr%s%d" % (c, s) for c in "AB" for s in range(N)]
               + ["%s%d" % (n, k) for n in ("za", "zb", "hr", "hd") for k in range(N)])
@@ -61,9 +63,7 @@ def _carriers(rc, group, topo):
 
 def _parts(src, on_chip, off_chip, topo):
     lo = _engines(topo.mask(src, off_chip))
-    hi = [e for e in _engines(topo.mask(src, on_chip)) if e not in lo]
-    return {"lo": lo, "hi": hi, "all": lo + hi,
-            "loL": lo[:len(lo) // 2], "loH": lo[len(lo) // 2:], "hiL": hi[:len(hi) // 2], "hiH": hi[len(hi) // 2:]}
+    return {"lo": lo, "hi": [e for e in _engines(topo.mask(src, on_chip)) if e not in lo]}
 
 
 def _view(T, piece, s):
@@ -83,21 +83,32 @@ def _arr(T, piece, s):
     return T.sem["arr%s%d" % (PIECES[piece][3], s)]
 
 
-def _after(group, s):
-    return [group[(s + k) % N] for k in range(1, N)]
+def _straight(to, group, s, topo):
+    after = [group[(s + k) % N] for k in range(1, N)]
+    if to == "ranks":
+        return after
+    return [d for d in after if topo.same_plane(topo.chip(group[s]), topo.chip(d))]
+
+
+def _left(piece, group, s, topo):
+    served = []
+    for _, trs in STEPS:
+        for p, to, _ in trs:
+            if p == piece and to in ("ranks", "plane"):
+                served += _straight(to, group, s, topo)
+    return [d for d in _straight("ranks", group, s, topo) if d not in served]
 
 
 def carrier_program(g, core, T, topo, group, s):
     rc = group[s]
     cs = _carriers(rc, group, topo)
-    dsts = _after(group, s)
-    give = _parts(rc, core, dsts[0], topo)
-    lo = _parts(core, rc, dsts[0], topo)["lo"]
     sent = 0
     for _, trs in STEPS:
         for piece, to, part in trs:
-            if to != "all" and cs[to[0]][to[1]] == core:
-                g.wait_ge(T.sem["in_" + piece], len(give[part]))
+            if to not in ("ranks", "plane") and cs[to[0]][to[1]] == core:
+                dsts = _left(piece, group, s, topo)
+                lo = _parts(core, rc, dsts[0], topo)["lo"]
+                g.wait_ge(T.sem["in_" + piece], len(_parts(rc, core, dsts[0], topo)[part]))
                 g.remote_dma_fused([_transfer(T, topo, piece, s, dsts, lo, _arr(T, piece, s))], local_sem=T.sem.sent)
                 sent += len(lo)
     if sent:
@@ -115,21 +126,20 @@ def rank_program(g, core, T, topo):
     S = T.sem
     own = me * SLOT
 
-    g.sync.dma_start(T.wb[:, 0:8 * NC], T.w1[:]).then_inc(S.ldw1, 16)
-    g.scalar.dma_start(T.wb[:, 8 * NC:12 * NC], T.w2[:]).then_inc(S.ldw2, 16)
-    g.sync.dma_start(T.xb[:], T.x[:]).then_inc(S.ldx, 16)
+    g.sync.dma_start(T.wb[:, 0:4 * NC], T.w1[:, 0:4 * NC]).then_inc(S.ld1, 16)
+    g.scalar.dma_start(T.wb[:, 4 * NC:8 * NC], T.w1[:, 4 * NC:8 * NC]).then_inc(S.ld2, 16)
+    g.sync.dma_start(T.wb[:, 8 * NC:12 * NC], T.w2[:]).then_inc(S.ld3, 16)
+    g.scalar.dma_start(T.xb[:], T.x[:]).then_inc(S.ldx, 16)
 
-    g.vector.wait_ge(S.ldw1, 16)
-    g.vector.quantize_mx(T.wq[:, own:own + 2 * NC], T.ws[:, own:own + 2 * NC], T.wb[:, 0:8 * NC]).then_inc(S.qw1, 1)
-    g.vector.wait_ge(S.ldw2, 16)
-    g.vector.quantize_mx(T.wq[:, own + 2 * NC:own + SLOT], T.ws[:, own + 2 * NC:own + SLOT],
-                         T.wb[:, 8 * NC:12 * NC]).then_inc(S.qw2, 1)
+    for t in range(3):
+        g.vector.wait_ge(S["ld%d" % (t + 1)], 16)
+        g.vector.quantize_mx(T.wq[:, own + t * NC:own + (t + 1) * NC], T.ws[:, own + t * NC:own + (t + 1) * NC],
+                             T.wb[:, 4 * t * NC:4 * (t + 1) * NC]).then_inc(S["qw%d" % (t + 1)], 1)
     g.vector.wait_ge(S.ldx, 16)
     g.vector.quantize_mx(T.xq[:], T.xs[:], T.xb[:]).then_inc(S.qx, 1)
 
     cs = _carriers(core, group, topo)
-    dsts = _after(group, me)
-    parts = _parts(core, (cs["far"] + cs["near"])[0], dsts[0], topo)
+    parts = _parts(core, (cs["far"] + cs["near"])[0], _straight("ranks", group, me, topo)[0], topo)
     stage, sent = 0, 0
     for st, trs in STEPS:
         while stage < st:
@@ -137,8 +147,8 @@ def rank_program(g, core, T, topo):
             g.wait_ge(S["qw%d" % stage], 1)
         call = []
         for piece, to, part in trs:
-            if to == "all":
-                call.append(_transfer(T, topo, piece, me, dsts, parts[part], _arr(T, piece, me)))
+            if to in ("ranks", "plane"):
+                call.append(_transfer(T, topo, piece, me, _straight(to, group, me, topo), parts[part], _arr(T, piece, me)))
             else:
                 call.append(_transfer(T, topo, piece, me, [cs[to[0]][to[1]]], parts[part], S["in_" + piece]))
             sent += len(parts[part])
@@ -146,11 +156,12 @@ def rank_program(g, core, T, topo):
     g.wait_ge(S.sent, sent)
 
     need = {"A": 0, "B": 0}
-    for _, trs in STEPS:
-        for piece, to, part in trs:
-            need[PIECES[piece][3]] += len(parts[part] if to == "all" else parts["lo"])
+    for piece in PIECES:
+        need[PIECES[piece][3]] += len(parts["lo"])
 
-    order = [(me - k) % N for k in range(N)]
+    before = [(me - k) % N for k in range(1, N)]
+    order = ([me] + [s for s in before if core in _straight("plane", group, s, topo)]
+             + [s for s in before if core not in _straight("plane", group, s, topo)])
 
     def bank(k, i):
         b = 512 * (2 * ZSET[k] + i)
@@ -160,6 +171,7 @@ def rank_program(g, core, T, topo):
         a = order[k] * SLOT
         if k == 0:
             g.tensor.wait_ge(S.qw1, 1)
+            g.tensor.wait_ge(S.qw2, 1)
             g.tensor.wait_ge(S.qx, 1)
         else:
             g.tensor.wait_ge(S["arrA%d" % order[k]], need["A"])
@@ -170,8 +182,8 @@ def rank_program(g, core, T, topo):
     def y(k, first, last):
         a = order[k] * SLOT + 2 * NC
         if k == 0:
-            g.tensor.wait_ge(S.qw2, 1)
-        elif need["B"]:
+            g.tensor.wait_ge(S.qw3, 1)
+        else:
             g.tensor.wait_ge(S["arrB%d" % order[k]], need["B"])
         g.tensor.wait_ge(S["hd%d" % k], 1)
         mm = g.tensor.matmul_mx(T.py[:, 0:NC], T.wq[:, a:a + NC], T.ws[:, a:a + NC],

from concourse.bass import DstId, RemoteDMATransfer
from concourse.mybir import dt, AluOpType, ActivationFunctionType

N = 4
NSIM = 112
NC = 128
SLOT = 3 * NC
C = 0.047

PIECES = {
    "w1a": ("c", 0, NC, "A"),
    "w1b": ("c", NC, 2 * NC, "A"),
    "w2": ("c", 2 * NC, 3 * NC, "B"),
    "sc": ("s", 0, 3 * NC, "A"),
}
STEPS = [
    (1, [("w1a", ("far", 0), "hi"), ("w1a", "plane", "lo")]),
    (2, [("w1b", ("far", 1), "hi"), ("w1b", "plane", "lo")]),
    (3, [("w2", ("near", 0), "hi")]),
    (3, [("sc", "ranks", "lo")]),
    (3, [("w2", "plane", "lo")]),
]
ZSET = [0, 1, 2, 0]

SCRATCH = {
    "wb": ("sbuf", [128, 4 * SLOT], "bfloat16"),
    "xb": ("sbuf", [128, 4 * NC], "bfloat16"),
    "wq": ("sbuf", [128, N * SLOT], "float8_e4m3fn_x4"),
    "ws": ("sbuf", [128, N * SLOT], "uint8"),
    "xq": ("sbuf", [128, NC], "float8_e4m3fn_x4"),
    "xs": ("sbuf", [128, NC], "uint8"),
    "hb": ("sbuf", [128, N * 4 * NC], "bfloat16"),
    "hq": ("sbuf", [128, N * NC], "float8_e4m3fn_x4"),
    "hs": ("sbuf", [128, N * NC], "uint8"),
    "yb": ("sbuf", [128, NC], "float32"),
    "pz": ("psum", [128, 512 * 6], "float32"),
    "py": ("psum", [128, 512], "float32"),
}
SEMAPHORES = (["ld1", "ld2", "ld3", "ldx", "qw1", "qw2", "qw3", "qx", "yd", "yc", "st", "sent"]
              + ["in_" + p for p in PIECES]
              + ["arr%s%d" % (c, s) for c in "AB" for s in range(N)]
              + ["%s%d" % (n, k) for n in ("za", "zb", "hr", "hd") for k in range(N)])


def _engines(mask):
    return [e for e in range(mask.bit_length()) if (mask >> e) & 1]


def _mask(es):
    m = 0
    for e in es:
        m |= 1 << e
    return m


def _carriers(rc, group, topo):
    others = [d for d in group if d != rc]
    cs = [c for c in range(NSIM) if topo.chip(c) == topo.chip(rc) and c not in group
          and all(topo.may_write(c, d) for d in others)]
    return {"far": [c for c in cs if topo.die(c) != topo.die(rc)],
            "near": [c for c in cs if topo.die(c) == topo.die(rc)]}


def _parts(src, on_chip, off_chip, topo):
    lo = _engines(topo.mask(src, off_chip))
    return {"lo": lo, "hi": [e for e in _engines(topo.mask(src, on_chip)) if e not in lo]}


def _view(T, piece, s):
    kind, a, b, _ = PIECES[piece]
    if kind == "c":
        return T.wq[:, s * SLOT + a:s * SLOT + b].bitcast(dt.uint8)
    return T.ws[:, s * SLOT + a:s * SLOT + b]


def _transfer(T, topo, piece, s, dsts, es, sem):
    return RemoteDMATransfer(dst_ids=[DstId(rid=topo.addr(d)[0], pnc=topo.addr(d)[1]) for d in dsts],
                             dma_engine_mask=_mask(es), remote_sem=sem,
                             srcs=[_view(T, piece, s)], dsts=[_view(T, piece, s) for d in dsts])


def _arr(T, piece, s):
    return T.sem["arr%s%d" % (PIECES[piece][3], s)]


def _straight(to, group, s, topo):
    after = [group[(s + k) % N] for k in range(1, N)]
    if to == "ranks":
        return after
    return [d for d in after if topo.same_plane(topo.chip(group[s]), topo.chip(d))]


def _left(piece, group, s, topo):
    served = []
    for _, trs in STEPS:
        for p, to, _ in trs:
            if p == piece and to in ("ranks", "plane"):
                served += _straight(to, group, s, topo)
    return [d for d in _straight("ranks", group, s, topo) if d not in served]


def carrier_program(g, core, T, topo, group, s):
    rc = group[s]
    cs = _carriers(rc, group, topo)
    sent = 0
    for _, trs in STEPS:
        for piece, to, part in trs:
            if to not in ("ranks", "plane") and cs[to[0]][to[1]] == core:
                dsts = _left(piece, group, s, topo)
                lo = _parts(core, rc, dsts[0], topo)["lo"]
                g.wait_ge(T.sem["in_" + piece], len(_parts(rc, core, dsts[0], topo)[part]))
                g.remote_dma_fused([_transfer(T, topo, piece, s, dsts, lo, _arr(T, piece, s))], local_sem=T.sem.sent)
                sent += len(lo)
    if sent:
        g.wait_ge(T.sem.sent, sent)


def rank_program(g, core, T, topo):
    group = [int(c) for c in T.cores]
    me = T.rank_of(core)
    if me is None:
        for s in range(N):
            if topo.chip(group[s]) == topo.chip(core):
                carrier_program(g, core, T, topo, group, s)
        return
    S = T.sem
    own = me * SLOT

    g.sync.dma_start(T.wb[:, 0:4 * NC], T.w1[:, 0:4 * NC]).then_inc(S.ld1, 16)
    g.scalar.dma_start(T.wb[:, 4 * NC:8 * NC], T.w1[:, 4 * NC:8 * NC]).then_inc(S.ld2, 16)
    g.sync.dma_start(T.wb[:, 8 * NC:12 * NC], T.w2[:]).then_inc(S.ld3, 16)
    g.scalar.dma_start(T.xb[:], T.x[:]).then_inc(S.ldx, 16)

    for t in range(3):
        g.vector.wait_ge(S["ld%d" % (t + 1)], 16)
        g.vector.quantize_mx(T.wq[:, own + t * NC:own + (t + 1) * NC], T.ws[:, own + t * NC:own + (t + 1) * NC],
                             T.wb[:, 4 * t * NC:4 * (t + 1) * NC]).then_inc(S["qw%d" % (t + 1)], 1)
    g.vector.wait_ge(S.ldx, 16)
    g.vector.quantize_mx(T.xq[:], T.xs[:], T.xb[:]).then_inc(S.qx, 1)

    cs = _carriers(core, group, topo)
    parts = _parts(core, (cs["far"] + cs["near"])[0], _straight("ranks", group, me, topo)[0], topo)
    stage, sent = 0, 0
    for st, trs in STEPS:
        while stage < st:
            stage += 1
            g.wait_ge(S["qw%d" % stage], 1)
        call = []
        for piece, to, part in trs:
            if to in ("ranks", "plane"):
                call.append(_transfer(T, topo, piece, me, _straight(to, group, me, topo), parts[part], _arr(T, piece, me)))
            else:
                call.append(_transfer(T, topo, piece, me, [cs[to[0]][to[1]]], parts[part], S["in_" + piece]))
            sent += len(parts[part])
        g.remote_dma_fused(call, local_sem=S.sent)
    g.wait_ge(S.sent, sent)

    need = {"A": 0, "B": 0}
    for piece in PIECES:
        need[PIECES[piece][3]] += len(parts["lo"])

    before = [(me - k) % N for k in range(1, N)]
    order = ([me] + [s for s in before if core in _straight("plane", group, s, topo)]
             + [s for s in before if core not in _straight("plane", group, s, topo)])

    def bank(k, i):
        b = 512 * (2 * ZSET[k] + i)
        return T.pz[:, b:b + NC]

    def z(k):
        a = order[k] * SLOT
        if k == 0:
            g.tensor.wait_ge(S.qw1, 1)
            g.tensor.wait_ge(S.qw2, 1)
            g.tensor.wait_ge(S.qx, 1)
        else:
            g.tensor.wait_ge(S["arrA%d" % order[k]], need["A"])
        for i, n in enumerate(("za", "zb")):
            g.tensor.matmul_mx(bank(k, i), T.wq[:, a + i * NC:a + (i + 1) * NC], T.ws[:, a + i * NC:a + (i + 1) * NC],
                               T.xq[:], T.xs[:], True, True).then_inc(S["%s%d" % (n, k)], 1)

    def y(k, first, last):
        a = order[k] * SLOT + 2 * NC
        if k == 0:
            g.tensor.wait_ge(S.qw3, 1)
        else:
            g.tensor.wait_ge(S["arrB%d" % order[k]], need["B"])
        g.tensor.wait_ge(S["hd%d" % k], 1)
        mm = g.tensor.matmul_mx(T.py[:, 0:NC], T.wq[:, a:a + NC], T.ws[:, a:a + NC],
                                T.hq[:, k * NC:(k + 1) * NC], T.hs[:, k * NC:(k + 1) * NC], first, last)
        if last:
            mm.then_inc(S.yd, 1)

    z(0)
    y(0, True, False)
    z(1)
    z(2)
    y(1, False, False)
    z(3)
    y(2, False, False)
    y(3, False, True)

    for k in range(N):
        h = k * 4 * NC
        hr = S["hr%d" % k]
        g.vector.wait_ge(S["za%d" % k], 1)
        g.vector.tensor_scalar(T.hb[:, h + 0:h + 4 * NC:4], bank(k, 0), C, 0.0, AluOpType.mult, AluOpType.max).then_inc(hr, 1)
        g.vector.tensor_scalar(T.hb[:, h + 1:h + 4 * NC:4], bank(k, 0), -C, 0.0, AluOpType.mult, AluOpType.max).then_inc(hr, 1)
        g.scalar.wait_ge(S["zb%d" % k], 1)
        g.scalar.activation(T.hb[:, h + 2:h + 4 * NC:4], bank(k, 1), ActivationFunctionType.Relu, scale=C).then_inc(hr, 1)
        g.scalar.activation(T.hb[:, h + 3:h + 4 * NC:4], bank(k, 1), ActivationFunctionType.Relu, scale=-C).then_inc(hr, 1)
        g.vector.wait_ge(hr, 4)
        g.vector.quantize_mx(T.hq[:, k * NC:(k + 1) * NC], T.hs[:, k * NC:(k + 1) * NC],
                             T.hb[:, h:h + 4 * NC]).then_inc(S["hd%d" % k], 1)

    g.vector.wait_ge(S.yd, 1)
    g.vector.tensor_copy(T.yb[:], T.py[:, 0:NC]).then_inc(S.yc, 1)
    g.sync.wait_ge(S.yc, 1)
    g.sync.dma_start(T.y[:], T.yb[:]).then_inc(S.st, 16)
    g.sync.wait_ge(S.st, 16)
